import numpy as np
import ml_dtypes


def mxq(x, axis, fmt="e4m3"):
    dtype, down = {"e4m3": (ml_dtypes.float8_e4m3fn, 7), "e5m2": (ml_dtypes.float8_e5m2, 14)}[fmt]
    v = np.moveaxis(np.asarray(x, np.float32).astype(ml_dtypes.bfloat16).astype(np.float64), axis, -1)
    blocks = v.reshape(v.shape[:-1] + (-1, 32))
    amax = np.abs(blocks).max(-1, keepdims=True)
    byte = np.maximum(np.where(amax > 0, np.frexp(amax)[1] - 1 + 127, 0) - down, 1)
    scale = np.exp2(byte - 127.0)
    codes = (blocks / scale).astype(np.float32).astype(dtype).astype(np.float64)
    return np.moveaxis((codes * scale).reshape(v.shape), -1, axis)


WIDE = False


def mx_kscale(k):
    if not WIDE:
        return np.ones(k)
    levels = np.array([10, -10, 5, -5, 0])
    if k % 512:
        return np.exp2(np.random.permutation(np.resize(levels, k // 32))).repeat(32)
    a = np.empty((k // 512, 16))
    for p in range(k // 512):
        a[p, :8] = np.random.permutation(np.resize(levels, 8))
        for g in range(8):
            far = levels[np.abs(levels - a[p, g]) >= 10]
            a[p, g + 8] = far[np.random.randint(len(far))]
    return np.exp2(a.ravel()).repeat(32)


def f64(x):
    return np.asarray(x).astype(np.float64)


def striped(idx):
    return np.tile(np.asarray(idx).reshape(-1, 16).T, (8, 1)).astype(np.uint16)


def unstriped(offs):
    return offs[:16].T.reshape(-1).astype(np.int64)


E2M1 = np.array([0.0, 0.5, 1.0, 1.5, 2.0, 3.0, 4.0, 6.0, -0.0, -0.5, -1.0, -1.5, -2.0, -3.0, -4.0, -6.0])


def pack_weight(w, fmt):
    k, n = w.shape
    w = f64(np.asarray(w, np.float32).astype(ml_dtypes.bfloat16)).reshape(k // 32, 32, n)
    amax = np.abs(w).max(1)
    if fmt == "e4m3":
        byte = np.frexp(amax)[1] - 1 + 127 - 7
    else:
        mant, ex = np.frexp(amax / 6.0)
        byte = np.where(mant > 0.5, ex, ex - 1) + 127
    byte = np.clip(np.where(amax > 0, byte, 1), 1, 254)
    scaled = (w * np.exp2(127.0 - byte)[:, None, :]).reshape(k, n).astype(np.float32)
    by_word = np.ascontiguousarray(scaled.reshape(k // 512, 128, 4, n).transpose(0, 1, 3, 2))
    if fmt == "e4m3":
        words = by_word.astype(ml_dtypes.float8_e4m3fn).view(np.uint8)
    else:
        c = by_word.astype(ml_dtypes.float4_e2m1fn).view(np.uint8) & 0xF
        words = (c[..., 0::2] | (c[..., 1::2] << 4)).reshape(k // 512, 128, 2 * n)
    return np.ascontiguousarray(words), np.ascontiguousarray(byte.astype(np.uint8).reshape(k // 512, 16, n))


def unpack_weight(words, scales, fmt):
    g, _, n = scales.shape
    words = np.ascontiguousarray(words).reshape(g, 128, n, -1)
    if fmt == "e4m3":
        vals = words.view(ml_dtypes.float8_e4m3fn).astype(np.float64)
    else:
        nib = np.empty((g, 128, n, 4), np.uint8)
        nib[..., 0::2] = words & 0xF
        nib[..., 1::2] = words >> 4
        vals = E2M1[nib]
    vals = vals * np.repeat(np.exp2(scales.astype(np.float64) - 127.0), 8, axis=1)[..., None]
    return vals.transpose(0, 1, 3, 2).reshape(g * 512, n)


def sigmoid(v):
    return 1.0 / (1.0 + np.exp(-v))


D, E, T, I, Q, G = 512, 512, 2048, 512, 128, 32


def setup_inputs():
    n = np.random.standard_normal
    idx = np.random.permutation(T)[:I]
    fd = mx_kscale(D)
    fe = mx_kscale(E)
    keysp = pack_weight(n((D, T)) / fd[:, None], "e4m3")
    valsp = pack_weight(n((E, T)) / fe[:, None], "e4m3")
    return {
        "query": (n((D, Q)) * 0.5 / np.sqrt(D) * fd[:, None]).astype(np.float32),
        "keys_words": keysp[0],
        "keys_scales": keysp[1],
        "helpf": (np.random.uniform(0.5, 1.5, (Q, 1))).astype(np.float32),
        "gout": (n((E, Q)) * 1 / np.sqrt(E) * fe[:, None]).astype(np.float32),
        "vals_words": valsp[0],
        "vals_scales": valsp[1],
        "old": (0.5 * n((Q, T))).astype(np.float32),
        "offs": striped(idx),
    }


def reference(query, keys_words, keys_scales, helpf, gout, vals_words, vals_scales, old, offs):
    idx = unstriped(offs)
    keysu = unpack_weight(keys_words, keys_scales, "e4m3")
    valsu = unpack_weight(vals_words, vals_scales, "e4m3")
    queryq = mxq(f64(query), 0, "e4m3")
    keysidxg = keysu[:, idx]
    a = queryq.T @ keysidxg
    m1 = a.reshape(Q, G, I // G).mean(axis=2)
    gt = sigmoid(m1 * 4.0)
    gr = np.repeat(gt, I // G, axis=1)
    s = a * (gr * f64(helpf) + 1.0)
    p = np.exp(s - np.max(s, axis=1, keepdims=True))
    z = np.sum(p, axis=1, keepdims=True)
    goutq = mxq(f64(gout), 0, "e4m3")
    valsidxg = valsu[:, idx]
    c0 = goutq.T @ valsidxg
    dz = np.sum(c0 * p / np.square(z) * (-1.0), axis=1, keepdims=True)
    dp = c0 / z + dz
    ds = dp * p
    dgr = ds * a * f64(helpf)
    dgt = dgr.reshape(Q, G, I // G).sum(axis=2)
    dm1 = dgt * gt * (1.0 - gt) * 4.0
    e1 = dm1 / 16.0
    r1 = np.repeat(e1, I // G, axis=1)
    da = ds * (gr * f64(helpf) + 1.0) + r1
    gs = da * 512.0
    gf = np.zeros((Q, T))
    gf[:, idx] = gs
    y = f64(old) + gf
    return y

@@ -1,0 +1,202 @@
+from contextlib import ExitStack
+
+import concourse.mybir as mybir
+
+F32 = mybir.dt.float32
+BF16 = mybir.dt.bfloat16
+I32 = mybir.dt.int32
+U32 = mybir.dt.uint32
+U16 = mybir.dt.uint16
+U8 = mybir.dt.uint8
+FP8X4 = mybir.dt.float8_e4m3fn_x4
+ALU = mybir.AluOpType
+ACT = mybir.ActivationFunctionType
+AXIS_X = mybir.AxisListType.X
+
+P = 128
+PACK = 4
+T = 2048
+SLOTS = 512
+PAGE = 16
+HALVES = 2
+HALF = SLOTS // HALVES
+HALF_PAGES = HALF // PAGE
+PAGES = SLOTS // PAGE
+STORE_WIDTHS = (512, 512, 512, 512)
+
+FLOPS = 2 * 2 * 512 * P * SLOTS
+
+
+def tile_attend_bpagemates_s_kernel(tc, query, keys_words, keys_scales, helpf, gout, vals_words, vals_scales, old, offs, out):
+    nc = tc.nc
+
+    def by_page(ap):
+        return ap.rearrange("p (g j) -> p g j", j=PAGE)
+
+    def spread(ap):
+        return ap.unsqueeze(2).to_broadcast([P, HALF_PAGES, PAGE])
+
+    def interleaved(ap):
+        return ap.rearrange("p (c i) t -> p c t i", i=4)
+
+    def planes(ap):
+        return ap.rearrange("p t (c i) -> p c t i", i=4)
+
+    with ExitStack() as ctx:
+        sb = ctx.enter_context(tc.tile_pool(name="sb", bufs=1))
+        psum = ctx.enter_context(tc.psum_pool(name="psum", bufs=1))
+
+        offsets = sb.tile([P, SLOTS // 16], U16, name="offsets")
+        nc.sync.dma_start(offsets[:], offs)
+        half_offsets = [offsets[:, h * HALF // 16 : (h + 1) * HALF // 16] for h in range(HALVES)]
+        cols = [slice(h * HALF, (h + 1) * HALF) for h in range(HALVES)]
+        pages = [slice(h * HALF_PAGES, (h + 1) * HALF_PAGES) for h in range(HALVES)]
+
+        def load_rows(src, name):
+            raw = sb.tile([P, PACK, P], F32, name=name, tag="raw")
+            nc.sync.dma_start(raw[:], src.rearrange("(p t) q -> p t q", t=PACK))
+            return raw
+
+        def load_words(src, name, tag):
+            pool_words = sb.tile([P, T], I32, name=name, tag=tag, align_bytes=64)
+            nc.sync.dma_start(pool_words[:], src[0].rearrange("p n t -> p (n t)").bitcast(I32))
+            return pool_words
+
+        def load_scales(src, name, tag, queues):
+            pool_scales = sb.tile([P, T], U8, name=name, tag=tag, align_bytes=64)
+            nc.vector.memset(pool_scales[:].bitcast(I32), 0)
+            rows = src[0].rearrange("(a r) n -> r a n", r=4)
+            for r, queue in enumerate(queues):
+                queue.dma_start(pool_scales[r:P:32, :].bitcast(I32), rows[r].bitcast(I32))
+            return pool_scales
+
+        def quantise(grouped, name):
+            codes = sb.tile([P, P], U32, name=name + "_codes", align_bytes=64)
+            scales = sb.tile([P, P], U8, name=name + "_scales", align_bytes=64)
+            nc.vector.quantize_mx(out=codes[:].bitcast(FP8X4), scales=scales[:], in_=grouped[:].rearrange("p q t -> p (q t)"))
+            return codes, scales
+
+        query_raw = load_rows(query, "query_raw")
+        keys_pool = load_words(keys_words, "keys_pool", "keys")
+        keys_pool_scales = load_scales(keys_scales, "keys_pool_scales", "keys_scales", [nc.scalar] * 4)
+        vals_pool = load_words(vals_words, "vals_pool", "vals")
+        help_col = sb.tile([P, 1], F32, name="help_col")
+        nc.gpsimd.dma_start(help_col[:], helpf)
+        vals_pool_scales = load_scales(vals_scales, "vals_pool_scales", "vals_scales", [nc.scalar, nc.scalar, nc.gpsimd, nc.gpsimd])
+
+        window = sb.tile([P, T], F32, name="window")
+        nc.vector.memset(window[:], 0.0)
+
+        consts = sb.tile([P, 4], F32, name="consts")
+        for j, (times, plus) in enumerate(((-0.5, 0.0), (-0.5, -1.0), (-32.0, 0.0), (32.0, 0.0))):
+            nc.scalar.activation(consts[:, j : j + 1], help_col[:], ACT.Copy, bias=plus, scale=times)
+
+        query_grouped = sb.tile([P, P, PACK], BF16, name="query_grouped", align_bytes=64)
+        nc.vector.tensor_copy(interleaved(query_grouped[:]), planes(query_raw[:]))
+        keys_scale_bytes = sb.tile([P, SLOTS], U8, name="keys_scale_bytes", align_bytes=64)
+        nc.vector.tensor_copy(keys_scale_bytes[:], keys_pool_scales[:].indirect(offsets[:]))
+        query_codes, query_scales = quantise(query_grouped, "query")
+        gout_raw = load_rows(gout, "gout_raw")
+
+        scores = []
+        for h in range(HALVES):
+            key_words = sb.tile([P, HALF], U32, name=f"key_words{h}", tag=("keys_scales", "key_words")[h], align_bytes=64)
+            nc.vector.tensor_copy(key_words[:], keys_pool[:].bitcast(U32).indirect(half_offsets[h]))
+            bank = psum.tile([P, HALF], F32, name=f"scores{h}")
+            nc.tensor.matmul_mx(
+                out=bank[:],
+                lhsT=query_codes[:].bitcast(FP8X4),
+                lhsT_scale=query_scales[:],
+                rhs=key_words[:].bitcast(FP8X4),
+                rhs_scale=keys_scale_bytes[:, cols[h]],
+                start=True,
+                stop=True,
+            )
+            scores.append(bank)
+
+
+        vals_scale_bytes = sb.tile([P, SLOTS], U8, name="vals_scale_bytes", tag="keys", align_bytes=64)
+        page_sums = sb.tile([P, PAGES], F32, name="page_sums")
+        tanhs = sb.tile([P, PAGES], F32, name="tanhs")
+        neg_factor = sb.tile([P, PAGES], F32, name="neg_factor")
+        for h in range(HALVES):
+            nc.vector.tensor_reduce(page_sums[:, pages[h]], by_page(scores[h][:]), AXIS_X, ALU.add)
+            nc.scalar.activation(tanhs[:, pages[h]], page_sums[:, pages[h]], ACT.Tanh, scale=0.125)
+            nc.scalar.activation(neg_factor[:, pages[h]], tanhs[:, pages[h]], ACT.Identity, bias=consts[:, 1:2], scale=consts[:, 0:1])
+            nc.vector.tensor_copy(vals_scale_bytes[:, cols[h]], vals_pool_scales[:].indirect(half_offsets[h]))
+
+        gout_grouped = sb.tile([P, P, PACK], BF16, name="gout_grouped", align_bytes=64)
+        nc.scalar.copy(interleaved(gout_grouped[:]), planes(gout_raw[:]))
+
+        page_coeffs = sb.tile([P, 2, PAGES], F32, name="page_coeffs")
+        squares = sb.tile([P, PAGES], F32, name="squares")
+        nc.scalar.activation(squares[:], tanhs[:], ACT.Square)
+        nc.scalar.activation(page_coeffs[:, 0, :], neg_factor[:], ACT.Copy, scale=-512.0)
+        nc.scalar.activation(page_coeffs[:, 1, :], squares[:], ACT.Identity, bias=consts[:, 3:4], scale=consts[:, 2:3])
+
+        neg_helped = sb.tile([P, SLOTS], F32, name="neg_helped")
+        weights = sb.tile([P, SLOTS], F32, name="weights")
+        least = sb.tile([P, HALVES], F32, name="least")
+        val_words = [sb.tile([P, HALF], U32, name=f"val_words{h}", align_bytes=64) for h in range(HALVES)]
+        nc.vector.tensor_copy(val_words[0][:], vals_pool[:].bitcast(U32).indirect(half_offsets[0]))
+        for h in range(HALVES):
+            nc.vector.tensor_tensor(by_page(neg_helped[:, cols[h]]), by_page(scores[h][:]), spread(neg_factor[:, pages[h]]), ALU.mult)
+        for h in range(HALVES):
+            nc.vector.tensor_scalar(
+                weights[:, cols[h]], neg_helped[:, cols[h]], 1.0, least[:, h - 1 : h] if h else None,
+                ALU.mult, ALU.min, accum_out=least[:, h : h + 1],
+            )
+        total = sb.tile([P, 1], F32, name="total")
+        nc.scalar.activation(weights[:], neg_helped[:], ACT.Exp, bias=least[:, HALVES - 1 : HALVES], scale=-1.0, accum_out=total[:])
+        gout_codes, gout_scales = quantise(gout_grouped, "gout")
+        nc.vector.tensor_copy(val_words[1][:], vals_pool[:].bitcast(U32).indirect(half_offsets[1]))
+
+        old_sb = sb.tile([P, T], F32, name="old_sb", tag="vals", align_bytes=64)
+        nc.sync.dma_start(old_sb[:], old)
+
+        reads = psum.tile([P, SLOTS], F32, name="reads")
+        for h in range(HALVES):
+            nc.tensor.matmul_mx(
+                out=reads[:, cols[h]],
+                lhsT=gout_codes[:].bitcast(FP8X4),
+                lhsT_scale=gout_scales[:],
+                rhs=val_words[h][:].bitcast(FP8X4),
+                rhs_scale=vals_scale_bytes[:, cols[h]],
+                start=True,
+                stop=True,
+            )
+
+        centred = sb.tile([P, SLOTS], F32, name="centred")
+        weighted_sum = sb.tile([P, 1], F32, name="weighted_sum")
+        inverse = sb.tile([P, 1], F32, name="inverse")
+        mean = sb.tile([P, 1], F32, name="mean")
+        nc.vector.scalar_tensor_tensor(centred[:], reads[:], 1.0, weights[:], ALU.mult, ALU.mult, accum_out=weighted_sum[:])
+        nc.vector.reciprocal(inverse[:], total[:])
+        nc.vector.tensor_scalar(mean[:], weighted_sum[:], inverse[:], None, ALU.mult)
+        coeffs = sb.tile([P, 2, PAGES], F32, name="coeffs")
+        nc.scalar.activation(coeffs[:], page_coeffs[:], ACT.Copy, scale=inverse[:])
+
+        products = sb.tile([P, SLOTS], F32, name="products")
+        product_sums = sb.tile([P, PAGES], F32, name="product_sums")
+        page_terms = sb.tile([P, PAGES], F32, name="page_terms")
+        direct = [sb.tile([P, HALF], F32, name=f"direct{h}") for h in range(HALVES)]
+        shared = [sb.tile([P, HALF], F32, name=f"shared{h}") for h in range(HALVES)]
+        for h in range(HALVES):
+            nc.vector.scalar_tensor_tensor(centred[:, cols[h]], reads[:, cols[h]], mean[:], weights[:, cols[h]], ALU.subtract, ALU.mult)
+        for h in range(HALVES):
+            nc.vector.tensor_tensor(products[:, cols[h]], centred[:, cols[h]], scores[h][:], ALU.mult)
+        for h in range(HALVES):
+            nc.vector.tensor_reduce(product_sums[:, pages[h]], by_page(products[:, cols[h]]), AXIS_X, ALU.add)
+        for h in range(HALVES):
+            nc.vector.tensor_tensor(page_terms[:, pages[h]], product_sums[:, pages[h]], coeffs[:, 1, pages[h]], ALU.mult)
+            nc.scalar.copy(by_page(shared[h][:]), spread(page_terms[:, pages[h]]))
+            nc.vector.tensor_tensor(by_page(direct[h][:]), by_page(centred[:, cols[h]]), spread(coeffs[:, 0, pages[h]]), ALU.mult)
+        for h in range(HALVES):
+            nc.vector.tensor_tensor(window[:].indirect(half_offsets[h]), direct[h][:], shared[h][:], ALU.add)
+
+        start = 0
+        for width in STORE_WIDTHS:
+            part = slice(start, start + width)
+            nc.vector.tensor_tensor(old_sb[:, part], old_sb[:, part], window[:, part], ALU.add)
+            nc.sync.dma_start(out[:, part], old_sb[:, part])
+            start = start + width

@@ -22,7 +22,7 @@ HALVES = 2
 HALF = SLOTS // HALVES
 HALF_PAGES = HALF // PAGE
 PAGES = SLOTS // PAGE
-STORE_WIDTHS = (512, 512, 512, 512)
+STORE_WIDTHS = (256,) * 8
 
 FLOPS = 2 * 2 * 512 * P * SLOTS
 
@@ -44,6 +44,7 @@ def tile_attend_bpagemates_s_kernel(tc, query, keys_words, keys_scales, helpf, g
 
     with ExitStack() as ctx:
         sb = ctx.enter_context(tc.tile_pool(name="sb", bufs=1))
+        reused = ctx.enter_context(tc.tile_pool(name="reused", bufs=1))
         psum = ctx.enter_context(tc.psum_pool(name="psum", bufs=1))
 
         offsets = sb.tile([P, SLOTS // 16], U16, name="offsets")
@@ -52,23 +53,21 @@ def tile_attend_bpagemates_s_kernel(tc, query, keys_words, keys_scales, helpf, g
         cols = [slice(h * HALF, (h + 1) * HALF) for h in range(HALVES)]
         pages = [slice(h * HALF_PAGES, (h + 1) * HALF_PAGES) for h in range(HALVES)]
 
-        def load_rows(src, name):
-            raw = sb.tile([P, PACK, P], F32, name=name, tag="raw")
+        def load_rows(src, name, tag):
+            raw = sb.tile([P, PACK, P], F32, name=name, tag=tag, align_bytes=64)
             nc.sync.dma_start(raw[:], src.rearrange("(p t) q -> p t q", t=PACK))
             return raw
 
-        def load_words(src, name, tag):
+        def load_words(src, name, tag, queue):
             pool_words = sb.tile([P, T], I32, name=name, tag=tag, align_bytes=64)
-            nc.sync.dma_start(pool_words[:], src[0].rearrange("p n t -> p (n t)").bitcast(I32))
+            queue.dma_start(pool_words[:], src[0].rearrange("p n t -> p (n t)").bitcast(I32))
             return pool_words
 
-        def load_scales(src, name, tag, queues):
-            pool_scales = sb.tile([P, T], U8, name=name, tag=tag, align_bytes=64)
-            nc.vector.memset(pool_scales[:].bitcast(I32), 0)
+        def load_scales(src, pool_scales):
+            nc.gpsimd.memset(pool_scales[:].bitcast(I32), 0)
             rows = src[0].rearrange("(a r) n -> r a n", r=4)
-            for r, queue in enumerate(queues):
-                queue.dma_start(pool_scales[r:P:32, :].bitcast(I32), rows[r].bitcast(I32))
-            return pool_scales
+            for r in range(4):
+                nc.sync.dma_start(pool_scales[r:P:32, :].bitcast(I32), rows[r].bitcast(I32))
 
         def quantise(grouped, name):
             codes = sb.tile([P, P], U32, name=name + "_codes", align_bytes=64)
@@ -76,27 +75,29 @@ def tile_attend_bpagemates_s_kernel(tc, query, keys_words, keys_scales, helpf, g
             nc.vector.quantize_mx(out=codes[:].bitcast(FP8X4), scales=scales[:], in_=grouped[:].rearrange("p q t -> p (q t)"))
             return codes, scales
 
-        query_raw = load_rows(query, "query_raw")
-        keys_pool = load_words(keys_words, "keys_pool", "keys")
-        keys_pool_scales = load_scales(keys_scales, "keys_pool_scales", "keys_scales", [nc.scalar] * 4)
-        vals_pool = load_words(vals_words, "vals_pool", "vals")
+        query_raw = load_rows(query, "query_raw", "gout")
+        keys_pool_scales = sb.tile([P, T], U8, name="keys_pool_scales", tag="keys_scales", align_bytes=64)
+        load_scales(keys_scales, keys_pool_scales)
+        keys_pool = load_words(keys_words, "keys_pool", "keys", nc.sync)
         help_col = sb.tile([P, 1], F32, name="help_col")
-        nc.gpsimd.dma_start(help_col[:], helpf)
-        vals_pool_scales = load_scales(vals_scales, "vals_pool_scales", "vals_scales", [nc.scalar, nc.scalar, nc.gpsimd, nc.gpsimd])
+        nc.scalar.dma_start(help_col[:], helpf)
+        vals_pool_scales = reused.tile([P, T], U8, name="vals_pool_scales", offset=0, align_bytes=64)
+        load_scales(vals_scales, vals_pool_scales)
 
         window = sb.tile([P, T], F32, name="window")
         nc.vector.memset(window[:], 0.0)
 
         consts = sb.tile([P, 4], F32, name="consts")
-        for j, (times, plus) in enumerate(((-0.5, 0.0), (-0.5, -1.0), (-32.0, 0.0), (32.0, 0.0))):
+        for j, (times, plus) in enumerate(((-0.5, 0.0), (-0.5, -1.0), (0.0625, 0.0), (-0.0625, 0.0))):
             nc.scalar.activation(consts[:, j : j + 1], help_col[:], ACT.Copy, bias=plus, scale=times)
 
-        query_grouped = sb.tile([P, P, PACK], BF16, name="query_grouped", align_bytes=64)
+        query_grouped = sb.tile([P, P, PACK], BF16, name="query_grouped", tag="vals", align_bytes=64)
         nc.vector.tensor_copy(interleaved(query_grouped[:]), planes(query_raw[:]))
         keys_scale_bytes = sb.tile([P, SLOTS], U8, name="keys_scale_bytes", align_bytes=64)
         nc.vector.tensor_copy(keys_scale_bytes[:], keys_pool_scales[:].indirect(offsets[:]))
         query_codes, query_scales = quantise(query_grouped, "query")
-        gout_raw = load_rows(gout, "gout_raw")
+        gout_raw = load_rows(gout, "gout_raw", "gout")
+        vals_pool = load_words(vals_words, "vals_pool", "vals", nc.scalar)
 
         scores = []
         for h in range(HALVES):
@@ -115,49 +116,57 @@ def tile_attend_bpagemates_s_kernel(tc, query, keys_words, keys_scales, helpf, g
             scores.append(bank)
 
 
-        vals_scale_bytes = sb.tile([P, SLOTS], U8, name="vals_scale_bytes", tag="keys", align_bytes=64)
-        page_sums = sb.tile([P, PAGES], F32, name="page_sums")
+        vals_scale_bytes = sb.tile([P, SLOTS], U8, name="vals_scale_bytes", align_bytes=64)
+        nc.vector.tensor_copy(vals_scale_bytes[:], vals_pool_scales[:].indirect(offsets[:]))
+        gout_grouped = sb.tile([P, P, PACK], BF16, name="gout_grouped", tag="gout_grouped", align_bytes=64)
+        nc.scalar.copy(interleaved(gout_grouped[:]), planes(gout_raw[:]))
+
+        page_sums = reused.tile([P, PAGES], F32, name="page_sums", offset=0)
         tanhs = sb.tile([P, PAGES], F32, name="tanhs")
-        neg_factor = sb.tile([P, PAGES], F32, name="neg_factor")
+        neg_factor = [
+            reused.tile([P, HALF_PAGES], F32, name="neg_factor0", offset=2048),
+            sb.tile([P, HALF_PAGES], F32, name="neg_factor1"),
+        ]
         for h in range(HALVES):
             nc.vector.tensor_reduce(page_sums[:, pages[h]], by_page(scores[h][:]), AXIS_X, ALU.add)
             nc.scalar.activation(tanhs[:, pages[h]], page_sums[:, pages[h]], ACT.Tanh, scale=0.125)
-            nc.scalar.activation(neg_factor[:, pages[h]], tanhs[:, pages[h]], ACT.Identity, bias=consts[:, 1:2], scale=consts[:, 0:1])
-            nc.vector.tensor_copy(vals_scale_bytes[:, cols[h]], vals_pool_scales[:].indirect(half_offsets[h]))
-
-        gout_grouped = sb.tile([P, P, PACK], BF16, name="gout_grouped", align_bytes=64)
-        nc.scalar.copy(interleaved(gout_grouped[:]), planes(gout_raw[:]))
-
-        page_coeffs = sb.tile([P, 2, PAGES], F32, name="page_coeffs")
+            nc.scalar.activation(neg_factor[h][:], tanhs[:, pages[h]], ACT.Identity, bias=consts[:, 1:2], scale=consts[:, 0:1])
         squares = sb.tile([P, PAGES], F32, name="squares")
+        gate_slope = sb.tile([P, PAGES], F32, name="gate_slope")
         nc.scalar.activation(squares[:], tanhs[:], ACT.Square)
-        nc.scalar.activation(page_coeffs[:, 0, :], neg_factor[:], ACT.Copy, scale=-512.0)
-        nc.scalar.activation(page_coeffs[:, 1, :], squares[:], ACT.Identity, bias=consts[:, 3:4], scale=consts[:, 2:3])
+        nc.scalar.activation(gate_slope[:], squares[:], ACT.Identity, bias=consts[:, 3:4], scale=consts[:, 2:3])
+        factor = sb.tile([P, PAGES], F32, name="factor")
+        nc.scalar.activation(factor[:], tanhs[:], ACT.Identity, bias=consts[:, 1:2], scale=consts[:, 0:1])
 
-        neg_helped = sb.tile([P, SLOTS], F32, name="neg_helped")
-        weights = sb.tile([P, SLOTS], F32, name="weights")
-        least = sb.tile([P, HALVES], F32, name="least")
-        val_words = [sb.tile([P, HALF], U32, name=f"val_words{h}", align_bytes=64) for h in range(HALVES)]
+        val_words = [
+            reused.tile([P, HALF], U32, name="val_words0", offset=1024, align_bytes=64),
+        ]
         nc.vector.tensor_copy(val_words[0][:], vals_pool[:].bitcast(U32).indirect(half_offsets[0]))
-        for h in range(HALVES):
-            nc.vector.tensor_tensor(by_page(neg_helped[:, cols[h]]), by_page(scores[h][:]), spread(neg_factor[:, pages[h]]), ALU.mult)
-        for h in range(HALVES):
-            nc.vector.tensor_scalar(
-                weights[:, cols[h]], neg_helped[:, cols[h]], 1.0, least[:, h - 1 : h] if h else None,
-                ALU.mult, ALU.min, accum_out=least[:, h : h + 1],
-            )
-        total = sb.tile([P, 1], F32, name="total")
-        nc.scalar.activation(weights[:], neg_helped[:], ACT.Exp, bias=least[:, HALVES - 1 : HALVES], scale=-1.0, accum_out=total[:])
         gout_codes, gout_scales = quantise(gout_grouped, "gout")
-        nc.vector.tensor_copy(val_words[1][:], vals_pool[:].bitcast(U32).indirect(half_offsets[1]))
 
-        old_sb = sb.tile([P, T], F32, name="old_sb", tag="vals", align_bytes=64)
-        nc.sync.dma_start(old_sb[:], old)
-
-        reads = psum.tile([P, SLOTS], F32, name="reads")
+        neg_helped_tile = sb.tile([P, SLOTS], F32, name="neg_helped")
+        neg_helped = neg_helped_tile[:]
         for h in range(HALVES):
+            nc.vector.tensor_tensor(by_page(neg_helped[:, cols[h]]), by_page(scores[h][:]), spread(neg_factor[h][:]), ALU.mult)
+        val_words.append(reused.tile([P, HALF], U32, name="val_words1", offset=2048, align_bytes=64))
+        nc.vector.tensor_copy(val_words[1][:], vals_pool[:].bitcast(U32).indirect(half_offsets[1]))
+        least = sb.tile([P, 1], F32, name="least")
+        nc.vector.tensor_reduce(least[:], neg_helped, AXIS_X, ALU.min)
+        sloped = sb.tile([P, SLOTS], F32, name="sloped", tag="vals", align_bytes=64)
+        for h in range(HALVES):
+            nc.vector.tensor_tensor(by_page(sloped[:, cols[h]]), by_page(scores[h][:]), spread(gate_slope[:, pages[h]]), ALU.mult)
+        weights = sb.tile([P, SLOTS], F32, name="weights")
+        totals = sb.tile([P, HALVES], F32, name="totals")
+        total = sb.tile([P, 1], F32, name="total")
+        for h in range(HALVES):
+            nc.scalar.activation(weights[:, cols[h]], neg_helped[:, cols[h]], ACT.Exp, bias=least[:], scale=-1.0, accum_out=totals[:, h : h + 1])
+        nc.scalar.activation(total[:], totals[:, 0:1], ACT.Identity, bias=totals[:, 1:2])
+
+        reads = []
+        for h in range(HALVES):
+            bank = psum.tile([P, HALF], F32, name=f"reads{h}")
             nc.tensor.matmul_mx(
-                out=reads[:, cols[h]],
+                out=bank[:],
                 lhsT=gout_codes[:].bitcast(FP8X4),
                 lhsT_scale=gout_scales[:],
                 rhs=val_words[h][:].bitcast(FP8X4),
@@ -165,38 +174,47 @@ def tile_attend_bpagemates_s_kernel(tc, query, keys_words, keys_scales, helpf, g
                 start=True,
                 stop=True,
             )
+            reads.append(bank)
+
+        old_sb = sb.tile([P, T], F32, name="old_sb", tag="gout_grouped", align_bytes=64)
+        nc.sync.dma_start(old_sb[:], old)
 
         centred = sb.tile([P, SLOTS], F32, name="centred")
-        weighted_sum = sb.tile([P, 1], F32, name="weighted_sum")
+        weighted_sums = sb.tile([P, HALVES], F32, name="weighted_sums")
         inverse = sb.tile([P, 1], F32, name="inverse")
         mean = sb.tile([P, 1], F32, name="mean")
-        nc.vector.scalar_tensor_tensor(centred[:], reads[:], 1.0, weights[:], ALU.mult, ALU.mult, accum_out=weighted_sum[:])
+        for h in range(HALVES):
+            nc.vector.scalar_tensor_tensor(
+                centred[:, cols[h]], reads[h][:], 1.0, weights[:, cols[h]], ALU.mult, ALU.mult, accum_out=weighted_sums[:, h : h + 1]
+            )
         nc.vector.reciprocal(inverse[:], total[:])
-        nc.vector.tensor_scalar(mean[:], weighted_sum[:], inverse[:], None, ALU.mult)
-        coeffs = sb.tile([P, 2, PAGES], F32, name="coeffs")
-        nc.scalar.activation(coeffs[:], page_coeffs[:], ACT.Copy, scale=inverse[:])
+        row_scale = sb.tile([P, 1], F32, name="row_scale")
+        nc.scalar.activation(row_scale[:], inverse[:], ACT.Copy, scale=-512.0)
+
+        weighted_slope = sb.tile([P, SLOTS], F32, name="weighted_slope")
+        nc.vector.tensor_tensor(weighted_slope[:, cols[0]], sloped[:, cols[0]], weights[:, cols[0]], ALU.mult)
+        nc.vector.tensor_scalar(mean[:], weighted_sums[:, 0:1], weighted_sums[:, 1:2], inverse[:], ALU.add, ALU.mult)
+        nc.vector.tensor_tensor(weighted_slope[:, cols[1]], sloped[:, cols[1]], weights[:, cols[1]], ALU.mult)
 
         products = sb.tile([P, SLOTS], F32, name="products")
-        product_sums = sb.tile([P, PAGES], F32, name="product_sums")
         page_terms = sb.tile([P, PAGES], F32, name="page_terms")
         direct = [sb.tile([P, HALF], F32, name=f"direct{h}") for h in range(HALVES)]
         shared = [sb.tile([P, HALF], F32, name=f"shared{h}") for h in range(HALVES)]
         for h in range(HALVES):
-            nc.vector.scalar_tensor_tensor(centred[:, cols[h]], reads[:, cols[h]], mean[:], weights[:, cols[h]], ALU.subtract, ALU.mult)
+            nc.vector.scalar_tensor_tensor(products[:, cols[h]], reads[h][:], mean[:], weighted_slope[:, cols[h]], ALU.subtract, ALU.mult)
         for h in range(HALVES):
-            nc.vector.tensor_tensor(products[:, cols[h]], centred[:, cols[h]], scores[h][:], ALU.mult)
-        for h in range(HALVES):
-            nc.vector.tensor_reduce(product_sums[:, pages[h]], by_page(products[:, cols[h]]), AXIS_X, ALU.add)
-        for h in range(HALVES):
-            nc.vector.tensor_tensor(page_terms[:, pages[h]], product_sums[:, pages[h]], coeffs[:, 1, pages[h]], ALU.mult)
+            nc.vector.tensor_reduce(page_terms[:, pages[h]], by_page(products[:, cols[h]]), AXIS_X, ALU.add)
             nc.scalar.copy(by_page(shared[h][:]), spread(page_terms[:, pages[h]]))
-            nc.vector.tensor_tensor(by_page(direct[h][:]), by_page(centred[:, cols[h]]), spread(coeffs[:, 0, pages[h]]), ALU.mult)
+        for h in range(HALVES):
+            nc.vector.scalar_tensor_tensor(centred[:, cols[h]], reads[h][:], mean[:], weights[:, cols[h]], ALU.subtract, ALU.mult)
+        for h in range(HALVES):
+            nc.vector.tensor_tensor(by_page(direct[h][:]), by_page(centred[:, cols[h]]), spread(factor[:, pages[h]]), ALU.mult)
         for h in range(HALVES):
             nc.vector.tensor_tensor(window[:].indirect(half_offsets[h]), direct[h][:], shared[h][:], ALU.add)
 
         start = 0
         for width in STORE_WIDTHS:
             part = slice(start, start + width)
-            nc.vector.tensor_tensor(old_sb[:, part], old_sb[:, part], window[:, part], ALU.add)
+            nc.vector.scalar_tensor_tensor(old_sb[:, part], window[:, part], row_scale[:], old_sb[:, part], ALU.mult, ALU.add)
             nc.sync.dma_start(out[:, part], old_sb[:, part])
             start = start + width

@@ -37,10 +37,7 @@ def tile_attend_bpagemates_s_kernel(tc, query, keys_words, keys_scales, helpf, g
         return ap.unsqueeze(2).to_broadcast([P, HALF_PAGES, PAGE])
 
     def interleaved(ap):
-        return ap.rearrange("p (c i) t -> p c t i", i=4)
-
-    def planes(ap):
-        return ap.rearrange("p t (c i) -> p c t i", i=4)
+        return ap.rearrange("p t q -> p q t")
 
     with ExitStack() as ctx:
         sb = ctx.enter_context(tc.tile_pool(name="sb", bufs=1))
@@ -53,15 +50,11 @@ def tile_attend_bpagemates_s_kernel(tc, query, keys_words, keys_scales, helpf, g
         cols = [slice(h * HALF, (h + 1) * HALF) for h in range(HALVES)]
         pages = [slice(h * HALF_PAGES, (h + 1) * HALF_PAGES) for h in range(HALVES)]
 
-        def load_rows(src, name, tag):
-            raw = sb.tile([P, PACK, P], F32, name=name, tag=tag, align_bytes=64)
+        def load_rows(src, raw):
             nc.sync.dma_start(raw[:], src.rearrange("(p t) q -> p t q", t=PACK))
-            return raw
 
-        def load_words(src, name, tag, queue):
-            pool_words = sb.tile([P, T], I32, name=name, tag=tag, align_bytes=64)
+        def load_words(src, pool_words, queue):
             queue.dma_start(pool_words[:], src[0].rearrange("p n t -> p (n t)").bitcast(I32))
-            return pool_words
 
         def load_scales(src, pool_scales):
             nc.gpsimd.memset(pool_scales[:].bitcast(I32), 0)
@@ -75,10 +68,12 @@ def tile_attend_bpagemates_s_kernel(tc, query, keys_words, keys_scales, helpf, g
             nc.vector.quantize_mx(out=codes[:].bitcast(FP8X4), scales=scales[:], in_=grouped[:].rearrange("p q t -> p (q t)"))
             return codes, scales
 
-        query_raw = load_rows(query, "query_raw", "gout")
+        query_raw = reused.tile([P, PACK, P], F32, name="query_raw", offset=4096 + 7168)
+        load_rows(query, query_raw)
         keys_pool_scales = sb.tile([P, T], U8, name="keys_pool_scales", tag="keys_scales", align_bytes=64)
         load_scales(keys_scales, keys_pool_scales)
-        keys_pool = load_words(keys_words, "keys_pool", "keys", nc.sync)
+        keys_pool = sb.tile([P, T], I32, name="keys_pool")
+        load_words(keys_words, keys_pool, nc.sync)
         help_col = sb.tile([P, 1], F32, name="help_col")
         nc.scalar.dma_start(help_col[:], helpf)
         vals_pool_scales = reused.tile([P, T], U8, name="vals_pool_scales", offset=0, align_bytes=64)
@@ -91,13 +86,15 @@ def tile_attend_bpagemates_s_kernel(tc, query, keys_words, keys_scales, helpf, g
         for j, (times, plus) in enumerate(((-0.5, 0.0), (-0.5, -1.0), (0.0625, 0.0), (-0.0625, 0.0))):
             nc.scalar.activation(consts[:, j : j + 1], help_col[:], ACT.Copy, bias=plus, scale=times)
 
-        query_grouped = sb.tile([P, P, PACK], BF16, name="query_grouped", tag="vals", align_bytes=64)
-        nc.vector.tensor_copy(interleaved(query_grouped[:]), planes(query_raw[:]))
+        query_grouped = sb.tile([P, P, PACK], BF16, name="query_grouped", align_bytes=64)
+        nc.vector.tensor_copy(query_grouped[:], interleaved(query_raw[:]))
         keys_scale_bytes = sb.tile([P, SLOTS], U8, name="keys_scale_bytes", align_bytes=64)
         nc.vector.tensor_copy(keys_scale_bytes[:], keys_pool_scales[:].indirect(offsets[:]))
         query_codes, query_scales = quantise(query_grouped, "query")
-        gout_raw = load_rows(gout, "gout_raw", "gout")
-        vals_pool = load_words(vals_words, "vals_pool", "vals", nc.scalar)
+        gout_raw = reused.tile([P, PACK, P], F32, name="gout_raw", offset=4096 + 8192)
+        load_rows(gout, gout_raw)
+        vals_pool = reused.tile([P, T], I32, name="vals_pool", offset=4096)
+        load_words(vals_words, vals_pool, nc.scalar)
 
         scores = []
         for h in range(HALVES):
@@ -119,7 +116,7 @@ def tile_attend_bpagemates_s_kernel(tc, query, keys_words, keys_scales, helpf, g
         vals_scale_bytes = sb.tile([P, SLOTS], U8, name="vals_scale_bytes", align_bytes=64)
         nc.vector.tensor_copy(vals_scale_bytes[:], vals_pool_scales[:].indirect(offsets[:]))
         gout_grouped = sb.tile([P, P, PACK], BF16, name="gout_grouped", tag="gout_grouped", align_bytes=64)
-        nc.scalar.copy(interleaved(gout_grouped[:]), planes(gout_raw[:]))
+        nc.scalar.copy(gout_grouped[:], interleaved(gout_raw[:]))
 
         page_sums = reused.tile([P, PAGES], F32, name="page_sums", offset=0)
         tanhs = sb.tile([P, PAGES], F32, name="tanhs")
@@ -152,7 +149,7 @@ def tile_attend_bpagemates_s_kernel(tc, query, keys_words, keys_scales, helpf, g
         nc.vector.tensor_copy(val_words[1][:], vals_pool[:].bitcast(U32).indirect(half_offsets[1]))
         least = sb.tile([P, 1], F32, name="least")
         nc.vector.tensor_reduce(least[:], neg_helped, AXIS_X, ALU.min)
-        sloped = sb.tile([P, SLOTS], F32, name="sloped", tag="vals", align_bytes=64)
+        sloped = reused.tile([P, SLOTS], F32, name="sloped", offset=4096)
         for h in range(HALVES):
             nc.vector.tensor_tensor(by_page(sloped[:, cols[h]]), by_page(scores[h][:]), spread(gate_slope[:, pages[h]]), ALU.mult)
         weights = sb.tile([P, SLOTS], F32, name="weights")
@@ -196,6 +193,9 @@ def tile_attend_bpagemates_s_kernel(tc, query, keys_words, keys_scales, helpf, g
         nc.vector.tensor_scalar(mean[:], weighted_sums[:, 0:1], weighted_sums[:, 1:2], inverse[:], ALU.add, ALU.mult)
         nc.vector.tensor_tensor(weighted_slope[:, cols[1]], sloped[:, cols[1]], weights[:, cols[1]], ALU.mult)
 
+        helped_weights = reused.tile([P, HALF], F32, name="helped_weights", offset=4096)
+        nc.gpsimd.tensor_tensor(by_page(helped_weights[:]), by_page(weights[:, cols[1]]), spread(factor[:, pages[1]]), ALU.mult)
+
         products = sb.tile([P, SLOTS], F32, name="products")
         page_terms = sb.tile([P, PAGES], F32, name="page_terms")
         direct = [sb.tile([P, HALF], F32, name=f"direct{h}") for h in range(HALVES)]
@@ -205,10 +205,10 @@ def tile_attend_bpagemates_s_kernel(tc, query, keys_words, keys_scales, helpf, g
         for h in range(HALVES):
             nc.vector.tensor_reduce(page_terms[:, pages[h]], by_page(products[:, cols[h]]), AXIS_X, ALU.add)
             nc.scalar.copy(by_page(shared[h][:]), spread(page_terms[:, pages[h]]))
-        for h in range(HALVES):
-            nc.vector.scalar_tensor_tensor(centred[:, cols[h]], reads[h][:], mean[:], weights[:, cols[h]], ALU.subtract, ALU.mult)
-        for h in range(HALVES):
-            nc.vector.tensor_tensor(by_page(direct[h][:]), by_page(centred[:, cols[h]]), spread(factor[:, pages[h]]), ALU.mult)
+            if h == 0:
+                nc.vector.scalar_tensor_tensor(centred[:, cols[0]], reads[0][:], mean[:], weights[:, cols[0]], ALU.subtract, ALU.mult)
+        nc.vector.tensor_tensor(by_page(direct[0][:]), by_page(centred[:, cols[0]]), spread(factor[:, pages[0]]), ALU.mult)
+        nc.vector.scalar_tensor_tensor(direct[1][:], reads[1][:], mean[:], helped_weights[:], ALU.subtract, ALU.mult)
         for h in range(HALVES):
             nc.vector.tensor_tensor(window[:].indirect(half_offsets[h]), direct[h][:], shared[h][:], ALU.add)
 

from contextlib import ExitStack

import concourse.mybir as mybir

F32 = mybir.dt.float32
BF16 = mybir.dt.bfloat16
I32 = mybir.dt.int32
U32 = mybir.dt.uint32
U16 = mybir.dt.uint16
U8 = mybir.dt.uint8
FP8X4 = mybir.dt.float8_e4m3fn_x4
ALU = mybir.AluOpType
ACT = mybir.ActivationFunctionType
AXIS_X = mybir.AxisListType.X

P = 128
PACK = 4
T = 2048
SLOTS = 512
PAGE = 16
HALVES = 2
HALF = SLOTS // HALVES
HALF_PAGES = HALF // PAGE
PAGES = SLOTS // PAGE
STORE_WIDTHS = (256,) * 8

FLOPS = 2 * 2 * 512 * P * SLOTS


def tile_attend_bpagemates_s_kernel(tc, query, keys_words, keys_scales, helpf, gout, vals_words, vals_scales, old, offs, out):
    nc = tc.nc

    def by_page(ap):
        return ap.rearrange("p (g j) -> p g j", j=PAGE)

    def spread(ap):
        return ap.unsqueeze(2).to_broadcast([P, HALF_PAGES, PAGE])

    def interleaved(ap):
        return ap.rearrange("p t q -> p q t")

    with ExitStack() as ctx:
        sb = ctx.enter_context(tc.tile_pool(name="sb", bufs=1))
        reused = ctx.enter_context(tc.tile_pool(name="reused", bufs=1))
        psum = ctx.enter_context(tc.psum_pool(name="psum", bufs=1))

        offsets = sb.tile([P, SLOTS // 16], U16, name="offsets")
        nc.sync.dma_start(offsets[:], offs)
        half_offsets = [offsets[:, h * HALF // 16 : (h + 1) * HALF // 16] for h in range(HALVES)]
        cols = [slice(h * HALF, (h + 1) * HALF) for h in range(HALVES)]
        pages = [slice(h * HALF_PAGES, (h + 1) * HALF_PAGES) for h in range(HALVES)]

        def load_rows(src, raw):
            nc.sync.dma_start(raw[:], src.rearrange("(p t) q -> p t q", t=PACK))

        def load_words(src, pool_words, queue):
            queue.dma_start(pool_words[:], src[0].rearrange("p n t -> p (n t)").bitcast(I32))

        def load_scales(src, pool_scales):
            nc.gpsimd.memset(pool_scales[:].bitcast(I32), 0)
            rows = src[0].rearrange("(a r) n -> r a n", r=4)
            for r in range(4):
                nc.sync.dma_start(pool_scales[r:P:32, :].bitcast(I32), rows[r].bitcast(I32))

        def quantise(grouped, name):
            codes = sb.tile([P, P], U32, name=name + "_codes", align_bytes=64)
            scales = sb.tile([P, P], U8, name=name + "_scales", align_bytes=64)
            nc.vector.quantize_mx(out=codes[:].bitcast(FP8X4), scales=scales[:], in_=grouped[:].rearrange("p q t -> p (q t)"))
            return codes, scales

        query_raw = reused.tile([P, PACK, P], F32, name="query_raw", offset=4096 + 7168)
        load_rows(query, query_raw)
        keys_pool_scales = sb.tile([P, T], U8, name="keys_pool_scales", tag="keys_scales", align_bytes=64)
        load_scales(keys_scales, keys_pool_scales)
        keys_pool = sb.tile([P, T], I32, name="keys_pool")
        load_words(keys_words, keys_pool, nc.sync)
        help_col = sb.tile([P, 1], F32, name="help_col")
        nc.scalar.dma_start(help_col[:], helpf)
        vals_pool_scales = reused.tile([P, T], U8, name="vals_pool_scales", offset=0, align_bytes=64)
        load_scales(vals_scales, vals_pool_scales)

        window = sb.tile([P, T], F32, name="window")
        nc.vector.memset(window[:], 0.0)

        consts = sb.tile([P, 4], F32, name="consts")
        for j, (times, plus) in enumerate(((-0.5, 0.0), (-0.5, -1.0), (0.0625, 0.0), (-0.0625, 0.0))):
            nc.scalar.activation(consts[:, j : j + 1], help_col[:], ACT.Copy, bias=plus, scale=times)

        query_grouped = sb.tile([P, P, PACK], BF16, name="query_grouped", align_bytes=64)
        nc.vector.tensor_copy(query_grouped[:], interleaved(query_raw[:]))
        keys_scale_bytes = sb.tile([P, SLOTS], U8, name="keys_scale_bytes", align_bytes=64)
        nc.vector.tensor_copy(keys_scale_bytes[:], keys_pool_scales[:].indirect(offsets[:]))
        query_codes, query_scales = quantise(query_grouped, "query")
        gout_raw = reused.tile([P, PACK, P], F32, name="gout_raw", offset=4096 + 8192)
        load_rows(gout, gout_raw)
        vals_pool = reused.tile([P, T], I32, name="vals_pool", offset=4096)
        load_words(vals_words, vals_pool, nc.scalar)

        scores = []
        for h in range(HALVES):
            key_words = sb.tile([P, HALF], U32, name=f"key_words{h}", tag=("keys_scales", "key_words")[h], align_bytes=64)
            nc.vector.tensor_copy(key_words[:], keys_pool[:].bitcast(U32).indirect(half_offsets[h]))
            bank = psum.tile([P, HALF], F32, name=f"scores{h}")
            nc.tensor.matmul_mx(
                out=bank[:],
                lhsT=query_codes[:].bitcast(FP8X4),
                lhsT_scale=query_scales[:],
                rhs=key_words[:].bitcast(FP8X4),
                rhs_scale=keys_scale_bytes[:, cols[h]],
                start=True,
                stop=True,
            )
            scores.append(bank)


        vals_scale_bytes = sb.tile([P, SLOTS], U8, name="vals_scale_bytes", align_bytes=64)
        nc.vector.tensor_copy(vals_scale_bytes[:], vals_pool_scales[:].indirect(offsets[:]))
        gout_grouped = sb.tile([P, P, PACK], BF16, name="gout_grouped", tag="gout_grouped", align_bytes=64)
        nc.scalar.copy(gout_grouped[:], interleaved(gout_raw[:]))

        page_sums = reused.tile([P, PAGES], F32, name="page_sums", offset=0)
        tanhs = sb.tile([P, PAGES], F32, name="tanhs")
        neg_factor = [
            reused.tile([P, HALF_PAGES], F32, name="neg_factor0", offset=2048),
            sb.tile([P, HALF_PAGES], F32, name="neg_factor1"),
        ]
        for h in range(HALVES):
            nc.vector.tensor_reduce(page_sums[:, pages[h]], by_page(scores[h][:]), AXIS_X, ALU.add)
            nc.scalar.activation(tanhs[:, pages[h]], page_sums[:, pages[h]], ACT.Tanh, scale=0.125)
            nc.scalar.activation(neg_factor[h][:], tanhs[:, pages[h]], ACT.Identity, bias=consts[:, 1:2], scale=consts[:, 0:1])
        squares = sb.tile([P, PAGES], F32, name="squares")
        gate_slope = sb.tile([P, PAGES], F32, name="gate_slope")
        nc.scalar.activation(squares[:], tanhs[:], ACT.Square)
        nc.scalar.activation(gate_slope[:], squares[:], ACT.Identity, bias=consts[:, 3:4], scale=consts[:, 2:3])
        factor = sb.tile([P, PAGES], F32, name="factor")
        nc.scalar.activation(factor[:], tanhs[:], ACT.Identity, bias=consts[:, 1:2], scale=consts[:, 0:1])

        val_words = [
            reused.tile([P, HALF], U32, name="val_words0", offset=1024, align_bytes=64),
        ]
        nc.vector.tensor_copy(val_words[0][:], vals_pool[:].bitcast(U32).indirect(half_offsets[0]))
        gout_codes, gout_scales = quantise(gout_grouped, "gout")

        neg_helped_tile = sb.tile([P, SLOTS], F32, name="neg_helped")
        neg_helped = neg_helped_tile[:]
        for h in range(HALVES):
            nc.vector.tensor_tensor(by_page(neg_helped[:, cols[h]]), by_page(scores[h][:]), spread(neg_factor[h][:]), ALU.mult)
        val_words.append(reused.tile([P, HALF], U32, name="val_words1", offset=2048, align_bytes=64))
        nc.vector.tensor_copy(val_words[1][:], vals_pool[:].bitcast(U32).indirect(half_offsets[1]))
        least = sb.tile([P, 1], F32, name="least")
        nc.vector.tensor_reduce(least[:], neg_helped, AXIS_X, ALU.min)
        sloped = reused.tile([P, SLOTS], F32, name="sloped", offset=4096)
        for h in range(HALVES):
            nc.vector.tensor_tensor(by_page(sloped[:, cols[h]]), by_page(scores[h][:]), spread(gate_slope[:, pages[h]]), ALU.mult)
        weights = sb.tile([P, SLOTS], F32, name="weights")
        totals = sb.tile([P, HALVES], F32, name="totals")
        total = sb.tile([P, 1], F32, name="total")
        for h in range(HALVES):
            nc.scalar.activation(weights[:, cols[h]], neg_helped[:, cols[h]], ACT.Exp, bias=least[:], scale=-1.0, accum_out=totals[:, h : h + 1])
        nc.scalar.activation(total[:], totals[:, 0:1], ACT.Identity, bias=totals[:, 1:2])

        reads = []
        for h in range(HALVES):
            bank = psum.tile([P, HALF], F32, name=f"reads{h}")
            nc.tensor.matmul_mx(
                out=bank[:],
                lhsT=gout_codes[:].bitcast(FP8X4),
                lhsT_scale=gout_scales[:],
                rhs=val_words[h][:].bitcast(FP8X4),
                rhs_scale=vals_scale_bytes[:, cols[h]],
                start=True,
                stop=True,
            )
            reads.append(bank)

        old_sb = sb.tile([P, T], F32, name="old_sb", tag="gout_grouped", align_bytes=64)
        nc.sync.dma_start(old_sb[:], old)

        centred = sb.tile([P, SLOTS], F32, name="centred")
        weighted_sums = sb.tile([P, HALVES], F32, name="weighted_sums")
        inverse = sb.tile([P, 1], F32, name="inverse")
        mean = sb.tile([P, 1], F32, name="mean")
        for h in range(HALVES):
            nc.vector.scalar_tensor_tensor(
                centred[:, cols[h]], reads[h][:], 1.0, weights[:, cols[h]], ALU.mult, ALU.mult, accum_out=weighted_sums[:, h : h + 1]
            )
        nc.vector.reciprocal(inverse[:], total[:])
        row_scale = sb.tile([P, 1], F32, name="row_scale")
        nc.scalar.activation(row_scale[:], inverse[:], ACT.Copy, scale=-512.0)

        weighted_slope = sb.tile([P, SLOTS], F32, name="weighted_slope")
        nc.vector.tensor_tensor(weighted_slope[:, cols[0]], sloped[:, cols[0]], weights[:, cols[0]], ALU.mult)
        nc.vector.tensor_scalar(mean[:], weighted_sums[:, 0:1], weighted_sums[:, 1:2], inverse[:], ALU.add, ALU.mult)
        nc.vector.tensor_tensor(weighted_slope[:, cols[1]], sloped[:, cols[1]], weights[:, cols[1]], ALU.mult)

        helped_weights = reused.tile([P, HALF], F32, name="helped_weights", offset=4096)
        nc.gpsimd.tensor_tensor(by_page(helped_weights[:]), by_page(weights[:, cols[1]]), spread(factor[:, pages[1]]), ALU.mult)

        products = sb.tile([P, SLOTS], F32, name="products")
        page_terms = sb.tile([P, PAGES], F32, name="page_terms")
        direct = [sb.tile([P, HALF], F32, name=f"direct{h}") for h in range(HALVES)]
        shared = [sb.tile([P, HALF], F32, name=f"shared{h}") for h in range(HALVES)]
        for h in range(HALVES):
            nc.vector.scalar_tensor_tensor(products[:, cols[h]], reads[h][:], mean[:], weighted_slope[:, cols[h]], ALU.subtract, ALU.mult)
        for h in range(HALVES):
            nc.vector.tensor_reduce(page_terms[:, pages[h]], by_page(products[:, cols[h]]), AXIS_X, ALU.add)
            nc.scalar.copy(by_page(shared[h][:]), spread(page_terms[:, pages[h]]))
            if h == 0:
                nc.vector.scalar_tensor_tensor(centred[:, cols[0]], reads[0][:], mean[:], weights[:, cols[0]], ALU.subtract, ALU.mult)
        nc.vector.tensor_tensor(by_page(direct[0][:]), by_page(centred[:, cols[0]]), spread(factor[:, pages[0]]), ALU.mult)
        nc.vector.scalar_tensor_tensor(direct[1][:], reads[1][:], mean[:], helped_weights[:], ALU.subtract, ALU.mult)
        for h in range(HALVES):
            nc.vector.tensor_tensor(window[:].indirect(half_offsets[h]), direct[h][:], shared[h][:], ALU.add)

        start = 0
        for width in STORE_WIDTHS:
            part = slice(start, start + width)
            nc.vector.scalar_tensor_tensor(old_sb[:, part], window[:, part], row_scale[:], old_sb[:, part], ALU.mult, ALU.add)
            nc.sync.dma_start(out[:, part], old_sb[:, part])
            start = start + width
